import numpy as np
import ml_dtypes


def mxq(x, axis, fmt="e4m3"):
    dtype, down = {"e4m3": (ml_dtypes.float8_e4m3fn, 7), "e5m2": (ml_dtypes.float8_e5m2, 14)}[fmt]
    v = np.moveaxis(np.asarray(x, np.float32).astype(ml_dtypes.bfloat16).astype(np.float64), axis, -1)
    blocks = v.reshape(v.shape[:-1] + (-1, 32))
    amax = np.abs(blocks).max(-1, keepdims=True)
    byte = np.maximum(np.where(amax > 0, np.frexp(amax)[1] - 1 + 127, 0) - down, 1)
    scale = np.exp2(byte - 127.0)
    codes = (blocks / scale).astype(np.float32).astype(dtype).astype(np.float64)
    return np.moveaxis((codes * scale).reshape(v.shape), -1, axis)


WIDE = False


def mx_kscale(k):
    if not WIDE:
        return np.ones(k)
    levels = np.array([10, -10, 5, -5, 0])
    if k % 512:
        return np.exp2(np.random.permutation(np.resize(levels, k // 32))).repeat(32)
    a = np.empty((k // 512, 16))
    for p in range(k // 512):
        a[p, :8] = np.random.permutation(np.resize(levels, 8))
        for g in range(8):
            far = levels[np.abs(levels - a[p, g]) >= 10]
            a[p, g + 8] = far[np.random.randint(len(far))]
    return np.exp2(a.ravel()).repeat(32)


def f64(x):
    return np.asarray(x).astype(np.float64)


def striped(idx):
    return np.tile(np.asarray(idx).reshape(-1, 16).T, (8, 1)).astype(np.uint16)


def unstriped(offs):
    return offs[:16].T.reshape(-1).astype(np.int64)


E2M1 = np.array([0.0, 0.5, 1.0, 1.5, 2.0, 3.0, 4.0, 6.0, -0.0, -0.5, -1.0, -1.5, -2.0, -3.0, -4.0, -6.0])


def pack_weight(w, fmt):
    k, n = w.shape
    w = f64(np.asarray(w, np.float32).astype(ml_dtypes.bfloat16)).reshape(k // 32, 32, n)
    amax = np.abs(w).max(1)
    if fmt == "e4m3":
        byte = np.frexp(amax)[1] - 1 + 127 - 7
    else:
        mant, ex = np.frexp(amax / 6.0)
        byte = np.where(mant > 0.5, ex, ex - 1) + 127
    byte = np.clip(np.where(amax > 0, byte, 1), 1, 254)
    scaled = (w * np.exp2(127.0 - byte)[:, None, :]).reshape(k, n).astype(np.float32)
    by_word = np.ascontiguousarray(scaled.reshape(k // 512, 128, 4, n).transpose(0, 1, 3, 2))
    if fmt == "e4m3":
        words = by_word.astype(ml_dtypes.float8_e4m3fn).view(np.uint8)
    else:
        c = by_word.astype(ml_dtypes.float4_e2m1fn).view(np.uint8) & 0xF
        words = (c[..., 0::2] | (c[..., 1::2] << 4)).reshape(k // 512, 128, 2 * n)
    return np.ascontiguousarray(words), np.ascontiguousarray(byte.astype(np.uint8).reshape(k // 512, 16, n))


def unpack_weight(words, scales, fmt):
    g, _, n = scales.shape
    words = np.ascontiguousarray(words).reshape(g, 128, n, -1)
    if fmt == "e4m3":
        vals = words.view(ml_dtypes.float8_e4m3fn).astype(np.float64)
    else:
        nib = np.empty((g, 128, n, 4), np.uint8)
        nib[..., 0::2] = words & 0xF
        nib[..., 1::2] = words >> 4
        vals = E2M1[nib]
    vals = vals * np.repeat(np.exp2(scales.astype(np.float64) - 127.0), 8, axis=1)[..., None]
    return vals.transpose(0, 1, 3, 2).reshape(g * 512, n)


def bf(x):
    return np.asarray(x, np.float32).astype(ml_dtypes.bfloat16)


def planes(Y):
    r, m = Y.shape
    b = f64(bf(Y)).reshape(r // 32, 32, m)
    amax = np.abs(b).max(1)
    byte = np.clip(np.where(amax > 0, np.frexp(amax)[1] - 1 + 127 - 7, 1), 1, 254)
    codes = (b * np.exp2(127.0 - byte)[:, None, :]).reshape(r, m).astype(np.float32).astype(ml_dtypes.float8_e4m3fn).view(np.uint8)
    words = codes.reshape(r // 512, 128, 4, m).transpose(0, 1, 3, 2)
    return np.ascontiguousarray(words), np.ascontiguousarray(byte.astype(np.uint8).reshape(r // 512, 16, m))


K, T, J, I, R, N = 1024, 2048, 1024, 512, 512, 512


def setup_inputs():
    n = np.random.standard_normal
    idx = np.random.permutation(T)[:J]
    idx2 = np.random.permutation(J)[:I]
    fk = mx_kscale(K)
    fr = mx_kscale(R)
    xqp = pack_weight(n((K, T)) / fk[:, None], "e2m1")
    wap = pack_weight(n((K, R)) * 1 / np.sqrt(K) * fk[:, None] * fr, "e4m3")
    wbp = pack_weight(n((R, N)) * 1 / np.sqrt(R) / fr[:, None], "e2m1")
    return {
        "xq_words": xqp[0],
        "xq_scales": xqp[1],
        "wa_words": wap[0],
        "wa_scales": wap[1],
        "wb_words": wbp[0],
        "wb_scales": wbp[1],
        "b": (np.random.uniform(-0.5, 0.5, (N, 1))).astype(np.float32),
        "offs": striped(idx),
        "offs2": striped(idx2),
    }


def reference(xq_words, xq_scales, wa_words, wa_scales, wb_words, wb_scales, b, offs, offs2):
    idx = unstriped(offs)
    idx2 = unstriped(offs2)
    xqu = unpack_weight(xq_words, xq_scales, "e2m1")
    wau = unpack_weight(wa_words, wa_scales, "e4m3")
    wbu = unpack_weight(wb_words, wb_scales, "e2m1")
    xqidxg = xqu[:, idx]
    a = wau.T @ xqidxg
    hid = np.maximum(a, 0.0)
    hs = hid[:, idx2]
    hsq = mxq(hs, 0, "e4m3")
    p = wbu.T @ hsq
    y = p + f64(b)
    words, scales = planes(y)
    return y, words, scales

@@ -1,0 +1,236 @@
+from contextlib import ExitStack
+
+import concourse.mybir as mybir
+
+K, T, J, I, R, N = 1024, 2048, 1024, 512, 512, 512
+FLOPS = 2 * K * R * J + 2 * R * N * I
+
+F32 = mybir.dt.float32
+BF16 = mybir.dt.bfloat16
+I32 = mybir.dt.int32
+U32 = mybir.dt.uint32
+U16 = mybir.dt.uint16
+U8 = mybir.dt.uint8
+FP8X4 = mybir.dt.float8_e4m3fn_x4
+FP4X4 = mybir.dt.float4_e2m1fn_x4
+ACT = mybir.ActivationFunctionType
+ALU = mybir.AluOpType
+
+P = 128
+PACK = 4
+PASSES = K // (P * PACK)
+HALF = 512
+CHUNKS = [(0, 256), (256, 128), (384, 128)]
+
+
+def tile_list_experts_second_opinion_pl_kernel(
+    tc, xq_words, xq_scales, wa_words, wa_scales, wb_words, wb_scales, b, offs, offs2, out_0, out_1, out_2
+):
+    nc = tc.nc
+    with ExitStack() as ctx:
+        keep = ctx.enter_context(tc.tile_pool(name="keep", bufs=1))
+        reuse = ctx.enter_context(tc.tile_pool(name="reuse", bufs=1))
+        psum = ctx.enter_context(tc.psum_pool(name="psum", bufs=1))
+
+        def sb(shape, dtype, name, tag=None):
+            return keep.tile(shape, dtype, name=name, tag=tag or name, align_bytes=64)
+
+        def placed(shape, dtype, name, offset):
+            return reuse.tile(shape, dtype, name=name, offset=offset, align_bytes=64)
+
+        list1 = keep.tile([P, J // 16], U16, name="list1")
+        list2 = keep.tile([P, I // 16], U16, name="list2")
+
+        xs_table = placed([P, T], U8, "xs_table", 0)
+        nc.vector.memset(xs_table[:].bitcast(I32), 0)
+        nc.sync.dma_start(xs_table[0:P:4, :].bitcast(I32), xq_scales.rearrange("z q t -> (z q) t").bitcast(I32))
+        nc.sync.dma_start(list1[:], offs)
+
+        wa_raw = placed([P, PASSES, R], I32, "wa_raw", 5120)
+        nc.scalar.dma_start(wa_raw[:], wa_words.rearrange("z p r t -> p z (r t)").bitcast(I32))
+        xw_table = [sb([P, T], U16, "xw_table%d" % z) for z in range(PASSES)]
+        for z in range(PASSES):
+            nc.scalar.dma_start(xw_table[z][:].bitcast(I32), xq_words[z].bitcast(I32))
+
+        was_raw = placed([P, PASSES * R], U8, "was_raw", 9216)
+        nc.vector.memset(was_raw[:].bitcast(I32), 0)
+        for q in range(4):
+            nc.sync.dma_start(
+                was_raw[32 * q : 32 * q + 4, :].rearrange("p (z r) -> p z r", z=PASSES).bitcast(I32),
+                wa_scales[:, 4 * q : 4 * q + 4, :].rearrange("z s r -> s z r").bitcast(I32),
+            )
+        xs_plane = [sb([P, J], U8, "xs_plane%d" % z) for z in range(PASSES)]
+        for z in range(PASSES):
+            nc.vector.memset(xs_plane[z][:].bitcast(I32), 0)
+        nc.sync.dma_start(list2[:], offs2)
+
+        bias = sb([P, PACK], F32, "bias")
+        nc.gpsimd.dma_start(bias[:], b.rearrange("(p t) o -> p (t o)", t=PACK))
+        wbs_raw = sb([P, N], U8, "wbs_raw")
+        nc.gpsimd.memset(wbs_raw[:].bitcast(I32), 0)
+        wb_raw = sb([P, 2 * N], U8, "wb_raw")
+        nc.gpsimd.dma_start(wb_raw[:].bitcast(I32), wb_words[0].bitcast(I32))
+        for q in range(4):
+            nc.gpsimd.dma_start(
+                wbs_raw[32 * q : 32 * q + 4, :].bitcast(I32), wb_scales[0, 4 * q : 4 * q + 4, :].bitcast(I32)
+            )
+
+        xs_picked = sb([P, J], U8, "xs_picked")
+        nc.vector.tensor_copy(xs_picked[:], xs_table[:].indirect(list1[:]))
+        for z in range(PASSES):
+            for s in range(4):
+                first = 64 * z + 4 * s
+                (nc.sync if z == 0 else nc.scalar).dma_start(
+                    xs_plane[z][s:P:32, :].bitcast(I32), xs_picked[first : first + 49 : 16, :].bitcast(I32)
+                )
+
+        wa_codes = placed([P, PASSES, PACK, P], I32, "wa_codes", 1024)
+        nc.vector.tensor_copy(
+            wa_codes[:].rearrange("p z t q -> p z q t"), wa_raw[:].rearrange("p z (q t) -> p z q t", t=PACK)
+        )
+        wa_plane = placed([P, PASSES, PACK, P], U8, "wa_plane", 0)
+        nc.vector.tensor_copy(
+            wa_plane[:].rearrange("p z t q -> p z q t"),
+            was_raw[:].rearrange("p (z q t) -> p z q t", z=PASSES, t=PACK),
+        )
+
+        hid = [sb([P, J], F32, "hid%d" % t) for t in range(PACK)]
+        xw_picked = placed([P, 2 * PASSES, HALF], U16, "xw_picked", 6144)
+        zero = placed([P, 1], F32, "zero", 10240)
+        zero_src = sb([P, 1], F32, "zero_src")
+        nc.vector.memset(zero_src[:], 0.0)
+        nc.scalar.activation(zero[:], zero_src[:], ACT.Relu)
+        for h in range(J // HALF):
+            cols = slice(h * HALF, (h + 1) * HALF)
+            picked = []
+            for z in range(PASSES):
+                words = xw_picked[:, 2 * h + z, :]
+                nc.vector.tensor_copy(
+                    words, xw_table[z][:].indirect(list1[:, h * HALF // 16 : (h + 1) * HALF // 16])
+                )
+                picked.append(words)
+            acc = [psum.tile([P, HALF], F32, name="acc%d%d" % (h, t), tag="bank%d" % (4 * h + t)) for t in range(PACK)]
+            if h == 0:
+                order = [(0, 0), (0, 1), (1, 0), (1, 1), (0, 2), (1, 2), (0, 3), (1, 3)]
+            else:
+                order = [(z, t) for t in range(PACK) for z in range(PASSES)]
+            for z, t in order:
+                nc.tensor.matmul_mx(
+                    out=acc[t][:],
+                    lhsT=wa_codes[:, z, t, :].bitcast(FP8X4),
+                    lhsT_scale=wa_plane[:, z, t, :],
+                    rhs=picked[z].bitcast(FP4X4),
+                    rhs_scale=xs_plane[z][:, cols],
+                    start=(z == 0),
+                    stop=(z == PASSES - 1),
+                )
+                if z == PASSES - 1:
+                    nc.scalar.activation(hid[t][:, cols], acc[t][:], ACT.Relu, bias=zero[:])
+
+        wb_codes = sb([P, PACK, P], U16, "wb_codes", tag="xw_table1")
+        nc.vector.tensor_copy(
+            wb_codes[:].rearrange("p t q -> p q t"), wb_raw[:].bitcast(U16).rearrange("p (q t) -> p q t", t=PACK)
+        )
+        wb_plane = sb([P, PACK, P], U8, "wb_plane", tag="xw_table0")
+        nc.vector.tensor_copy(
+            wb_plane[:].rearrange("p t q -> p q t"), wbs_raw[:].rearrange("p (q t) -> p q t", t=PACK)
+        )
+
+        y_codes = sb([P, I], U32, "y_codes")
+        y_plane = sb([P, I], U8, "y_plane")
+        out_rows = out_0.rearrange("(p t) i -> p t i", t=PACK)
+        out_words = out_1[0].rearrange("p i t -> p (i t)").bitcast(I32)
+        last = len(CHUNKS) - 1
+
+        hs_rows, hs_woven, hs_codes, hs_plane, banks, y = {}, {}, {}, {}, {}, {}
+
+        def gather(c):
+            i0, w = CHUNKS[c]
+            if c == 1:
+                hs_rows[c] = placed([P, PACK, w], BF16, "hs_rows1", 10240)
+            else:
+                hs_rows[c] = sb([P, PACK, w], BF16, "hs_rows%d" % c, tag="hs_rows0")
+            for t in range(PACK):
+                nc.vector.tensor_copy(hs_rows[c][:, t, :], hid[t][:].indirect(list2[:, i0 // 16 : (i0 + w) // 16]))
+
+        def weave(c):
+            i0, w = CHUNKS[c]
+            hs_woven[c] = sb([P, w, PACK], BF16, "hs_woven%d" % c)
+            dst = hs_woven[c][:].rearrange("p (g i) t -> p g t i", i=4)
+            src = hs_rows[c][:].rearrange("p t (g i) -> p g t i", i=4)
+            if c == last:
+                nc.vector.tensor_copy(dst, src)
+            else:
+                nc.scalar.copy(dst, src)
+
+        def multiply(c):
+            i0, w = CHUNKS[c]
+            hs_codes[c] = sb([P, w], U32, "hs_codes%d" % c)
+            hs_plane[c] = sb([P, w], U8, "hs_plane%d" % c)
+            nc.vector.quantize_mx(
+                out=hs_codes[c][:].bitcast(FP8X4), scales=hs_plane[c][:], in_=hs_woven[c][:].rearrange("p i t -> p (i t)")
+            )
+            per_bank = HALF // w
+            first_bank = i0 // P
+            banks[c] = [
+                psum.tile([P, per_bank, w], F32, name="res%d%d" % (c, u), tag="bank%d" % (first_bank + u))
+                for u in range(PACK // per_bank)
+            ]
+            for t in range(PACK):
+                nc.tensor.matmul_mx(
+                    out=banks[c][t // per_bank][:, t % per_bank, :],
+                    lhsT=wb_codes[:, t, :].bitcast(FP4X4),
+                    lhsT_scale=wb_plane[:, t, :],
+                    rhs=hs_codes[c][:].bitcast(FP8X4),
+                    rhs_scale=hs_plane[c][:],
+                    start=True,
+                    stop=True,
+                )
+
+        y_woven = {}
+
+        def drain(c):
+            i0, w = CHUNKS[c]
+            per_bank = HALF // w
+            y[c] = sb([P, PACK, w], F32, "y%d" % c)
+            for t in range(PACK):
+                nc.scalar.activation(
+                    y[c][:, t, :], banks[c][t // per_bank][:, t % per_bank, :], ACT.Identity, bias=bias[:, t : t + 1]
+                )
+            nc.sync.dma_start(out_rows[:, :, i0 : i0 + w], y[c][:])
+
+        def weave_y(c, dst):
+            nc.vector.tensor_copy(
+                dst.rearrange("p (g i) t -> p g t i", i=4), y[c][:].rearrange("p t (g i) -> p g t i", i=4)
+            )
+
+        def hand_on(i0, w, woven):
+            nc.vector.quantize_mx(
+                out=y_codes[:, i0 : i0 + w].bitcast(FP8X4),
+                scales=y_plane[:, i0 : i0 + w],
+                in_=woven.rearrange("p i t -> p (i t)"),
+            )
+            nc.sync.dma_start(out_words[:, i0 : i0 + w], y_codes[:, i0 : i0 + w].bitcast(I32))
+
+        gather(0)
+        weave(0)
+        gather(1)
+        weave(1)
+        multiply(0)
+        gather(2)
+        multiply(1)
+        weave(2)
+        multiply(2)
+        drain(0)
+        drain(1)
+        drain(2)
+        first = sb([P, 256, PACK], BF16, "y_woven0")
+        rest = sb([P, 256, PACK], BF16, "y_woven1")
+        weave_y(0, first[:])
+        weave_y(1, rest[:, 0:128, :])
+        hand_on(0, 256, first[:])
+        weave_y(2, rest[:, 128:256, :])
+        hand_on(256, 256, rest[:])
+        for q in range(4):
+            eng = nc.sync if q < 2 else nc.scalar
+            eng.dma_start(out_2[0, 4 * q : 4 * q + 4, :].bitcast(I32), y_plane[32 * q : 32 * q + 4, :].bitcast(I32))

@@ -43,75 +43,78 @@ def tile_list_experts_second_opinion_pl_kernel(
 
         xs_table = placed([P, T], U8, "xs_table", 0)
         nc.vector.memset(xs_table[:].bitcast(I32), 0)
-        nc.sync.dma_start(xs_table[0:P:4, :].bitcast(I32), xq_scales.rearrange("z q t -> (z q) t").bitcast(I32))
         nc.sync.dma_start(list1[:], offs)
-
-        wa_raw = placed([P, PASSES, R], I32, "wa_raw", 5120)
-        nc.scalar.dma_start(wa_raw[:], wa_words.rearrange("z p r t -> p z (r t)").bitcast(I32))
-        xw_table = [sb([P, T], U16, "xw_table%d" % z) for z in range(PASSES)]
-        for z in range(PASSES):
-            nc.scalar.dma_start(xw_table[z][:].bitcast(I32), xq_words[z].bitcast(I32))
-
-        was_raw = placed([P, PASSES * R], U8, "was_raw", 9216)
+        nc.sync.dma_start(list2[:], offs2)
+        nc.sync.dma_start(xs_table[0:P:4, :].bitcast(I32), xq_scales.rearrange("z v t -> v z t").bitcast(I32))
+        was_raw = placed([P, PASSES * R], U8, "was_raw", 5632)
         nc.vector.memset(was_raw[:].bitcast(I32), 0)
         for q in range(4):
             nc.sync.dma_start(
                 was_raw[32 * q : 32 * q + 4, :].rearrange("p (z r) -> p z r", z=PASSES).bitcast(I32),
                 wa_scales[:, 4 * q : 4 * q + 4, :].rearrange("z s r -> s z r").bitcast(I32),
             )
-        xs_plane = [sb([P, J], U8, "xs_plane%d" % z) for z in range(PASSES)]
-        for z in range(PASSES):
-            nc.vector.memset(xs_plane[z][:].bitcast(I32), 0)
-        nc.sync.dma_start(list2[:], offs2)
+        zero = placed([P, 1], F32, "zero", 20992)
+        zero_a = reuse.tile([P, 16], F32, name="zero_a", offset=10752 - 32, align_bytes=32)
+        zero_b = reuse.tile([P, 16], F32, name="zero_b", offset=18944 - 32, align_bytes=32)
+        nc.vector.memset(zero_a[:], 0.0)
+        nc.vector.memset(zero_b[:], 0.0)
+        nc.scalar.activation(zero[:], zero_a[:, 0:1], ACT.Relu, bias=zero_b[:, 0:1])
 
+        wa_raw = placed([P, PASSES, R], I32, "wa_raw", 6656)
+        nc.sync.dma_start(wa_raw[:], wa_words.rearrange("z p r t -> p z (r t)").bitcast(I32))
+        xw_table = [placed([P, T], U16, "xw_table%d" % z, 10752 + 4096 * z) for z in range(PASSES)]
+        for z in range(PASSES):
+            nc.sync.dma_start(xw_table[z][:].bitcast(I32), xq_words[z].bitcast(I32))
+        xs_plane = sb([P, PASSES * J], U8, "xs_plane")
+        nc.vector.memset(xs_plane[:].bitcast(I32), 0)
         bias = sb([P, PACK], F32, "bias")
         nc.gpsimd.dma_start(bias[:], b.rearrange("(p t) o -> p (t o)", t=PACK))
-        wbs_raw = sb([P, N], U8, "wbs_raw")
-        nc.gpsimd.memset(wbs_raw[:].bitcast(I32), 0)
-        wb_raw = sb([P, 2 * N], U8, "wb_raw")
-        nc.gpsimd.dma_start(wb_raw[:].bitcast(I32), wb_words[0].bitcast(I32))
-        for q in range(4):
-            nc.gpsimd.dma_start(
-                wbs_raw[32 * q : 32 * q + 4, :].bitcast(I32), wb_scales[0, 4 * q : 4 * q + 4, :].bitcast(I32)
-            )
+        wb_raw = placed([P, N], U16, "wb_raw", 18944)
+        nc.sync.dma_start(wb_raw[:].bitcast(I32), wb_words[0].bitcast(I32))
 
         xs_picked = sb([P, J], U8, "xs_picked")
         nc.vector.tensor_copy(xs_picked[:], xs_table[:].indirect(list1[:]))
-        for z in range(PASSES):
-            for s in range(4):
-                first = 64 * z + 4 * s
-                (nc.sync if z == 0 else nc.scalar).dma_start(
-                    xs_plane[z][s:P:32, :].bitcast(I32), xs_picked[first : first + 49 : 16, :].bitcast(I32)
-                )
+        for q in range(4):
+            nc.scalar.dma_start(
+                xs_plane[32 * q : 32 * q + 4, :].rearrange("p (z j) -> p z j", z=PASSES).bitcast(I32),
+                xs_picked[32 * q : 32 * q + 32 : 4, :].bitcast(I32),
+            )
 
-        wa_codes = placed([P, PASSES, PACK, P], I32, "wa_codes", 1024)
-        nc.vector.tensor_copy(
-            wa_codes[:].rearrange("p z t q -> p z q t"), wa_raw[:].rearrange("p z (q t) -> p z q t", t=PACK)
-        )
-        wa_plane = placed([P, PASSES, PACK, P], U8, "wa_plane", 0)
+        wa_plane = placed([P, PASSES, PACK, P], U8, "wa_plane", 512)
         nc.vector.tensor_copy(
             wa_plane[:].rearrange("p z t q -> p z q t"),
             was_raw[:].rearrange("p (z q t) -> p z q t", z=PASSES, t=PACK),
         )
+        wa_codes = placed([P, PASSES, PACK, P], I32, "wa_codes", 1536)
+        nc.vector.tensor_copy(
+            wa_codes[:].rearrange("p z t q -> p z q t"), wa_raw[:].rearrange("p z (q t) -> p z q t", t=PACK)
+        )
+        wbs_raw = placed([P, N], U8, "wbs_raw", 0)
+        nc.vector.memset(wbs_raw[:].bitcast(I32), 0)
+        for q in range(4):
+            nc.sync.dma_start(
+                wbs_raw[32 * q : 32 * q + 4, :].bitcast(I32), wb_scales[0, 4 * q : 4 * q + 4, :].bitcast(I32)
+            )
 
         hid = [sb([P, J], F32, "hid%d" % t) for t in range(PACK)]
-        xw_picked = placed([P, 2 * PASSES, HALF], U16, "xw_picked", 6144)
-        zero = placed([P, 1], F32, "zero", 10240)
-        zero_src = sb([P, 1], F32, "zero_src")
-        nc.vector.memset(zero_src[:], 0.0)
-        nc.scalar.activation(zero[:], zero_src[:], ACT.Relu)
+        xw_picked = [placed([P, PASSES, HALF], U16, "xw_picked%d" % h, (5632, 18944)[h]) for h in range(2)]
         for h in range(J // HALF):
             cols = slice(h * HALF, (h + 1) * HALF)
             picked = []
+            if h == 1:
+                wb_codes = sb([P, PACK, P], U16, "wb_codes")
+                nc.vector.tensor_copy(
+                    wb_codes[:].rearrange("p t q -> p q t"), wb_raw[:].rearrange("p (q t) -> p q t", t=PACK)
+                )
             for z in range(PASSES):
-                words = xw_picked[:, 2 * h + z, :]
+                words = xw_picked[h][:, z, :]
                 nc.vector.tensor_copy(
                     words, xw_table[z][:].indirect(list1[:, h * HALF // 16 : (h + 1) * HALF // 16])
                 )
                 picked.append(words)
-            acc = [psum.tile([P, HALF], F32, name="acc%d%d" % (h, t), tag="bank%d" % (4 * h + t)) for t in range(PACK)]
+            acc = [psum.tile([P, HALF], F32, name="acc%d%d" % (h, t), tag="bank%d" % (t % 3 if h == 0 else 3 + t)) for t in range(PACK)]
             if h == 0:
-                order = [(0, 0), (0, 1), (1, 0), (1, 1), (0, 2), (1, 2), (0, 3), (1, 3)]
+                order = [(0, 0), (0, 1), (0, 2), (1, 0), (1, 1), (1, 2), (0, 3), (1, 3)]
             else:
                 order = [(z, t) for t in range(PACK) for z in range(PASSES)]
             for z, t in order:
@@ -120,18 +123,14 @@ def tile_list_experts_second_opinion_pl_kernel(
                     lhsT=wa_codes[:, z, t, :].bitcast(FP8X4),
                     lhsT_scale=wa_plane[:, z, t, :],
                     rhs=picked[z].bitcast(FP4X4),
-                    rhs_scale=xs_plane[z][:, cols],
+                    rhs_scale=xs_plane[:, z * J + h * HALF : z * J + (h + 1) * HALF],
                     start=(z == 0),
                     stop=(z == PASSES - 1),
                 )
                 if z == PASSES - 1:
                     nc.scalar.activation(hid[t][:, cols], acc[t][:], ACT.Relu, bias=zero[:])
 
-        wb_codes = sb([P, PACK, P], U16, "wb_codes", tag="xw_table1")
-        nc.vector.tensor_copy(
-            wb_codes[:].rearrange("p t q -> p q t"), wb_raw[:].bitcast(U16).rearrange("p (q t) -> p q t", t=PACK)
-        )
-        wb_plane = sb([P, PACK, P], U8, "wb_plane", tag="xw_table0")
+        wb_plane = placed([P, PACK, P], U8, "wb_plane", 15872)
         nc.vector.tensor_copy(
             wb_plane[:].rearrange("p t q -> p q t"), wbs_raw[:].rearrange("p (q t) -> p q t", t=PACK)
         )
@@ -147,7 +146,7 @@ def tile_list_experts_second_opinion_pl_kernel(
         def gather(c):
             i0, w = CHUNKS[c]
             if c == 1:
-                hs_rows[c] = placed([P, PACK, w], BF16, "hs_rows1", 10240)
+                hs_rows[c] = placed([P, PACK, w], BF16, "hs_rows1", 20992)
             else:
                 hs_rows[c] = sb([P, PACK, w], BF16, "hs_rows%d" % c, tag="hs_rows0")
             for t in range(PACK):
@@ -171,9 +170,9 @@ def tile_list_experts_second_opinion_pl_kernel(
                 out=hs_codes[c][:].bitcast(FP8X4), scales=hs_plane[c][:], in_=hs_woven[c][:].rearrange("p i t -> p (i t)")
             )
             per_bank = HALF // w
-            first_bank = i0 // P
+            first_bank = (7 + i0 // P) % 8
             banks[c] = [
-                psum.tile([P, per_bank, w], F32, name="res%d%d" % (c, u), tag="bank%d" % (first_bank + u))
+                psum.tile([P, per_bank, w], F32, name="res%d%d" % (c, u), tag="bank%d" % ((first_bank + u) % 8))
                 for u in range(PACK // per_bank)
             ]
             for t in range(PACK):

@@ -20,7 +20,7 @@ P = 128
 PACK = 4
 PASSES = K // (P * PACK)
 HALF = 512
-CHUNKS = [(0, 256), (256, 128), (384, 128)]
+CHUNKS = [(0, 128), (128, 128), (256, 128), (384, 128)]
 
 
 def tile_list_experts_second_opinion_pl_kernel(
@@ -54,28 +54,28 @@ def tile_list_experts_second_opinion_pl_kernel(
                 wa_scales[:, 4 * q : 4 * q + 4, :].rearrange("z s r -> s z r").bitcast(I32),
             )
         zero = placed([P, 1], F32, "zero", 20992)
-        zero_a = reuse.tile([P, 16], F32, name="zero_a", offset=10752 - 32, align_bytes=32)
-        zero_b = reuse.tile([P, 16], F32, name="zero_b", offset=18944 - 32, align_bytes=32)
-        nc.vector.memset(zero_a[:], 0.0)
-        nc.vector.memset(zero_b[:], 0.0)
+        zero_a = reuse.tile([P, 16], F32, name="zero_a", offset=8704 - 32, align_bytes=32)
+        zero_b = reuse.tile([P, 16], F32, name="zero_b", offset=16896 - 32, align_bytes=32)
+        nc.gpsimd.memset(zero_a[:], 0.0)
+        nc.gpsimd.memset(zero_b[:], 0.0)
         nc.scalar.activation(zero[:], zero_a[:, 0:1], ACT.Relu, bias=zero_b[:, 0:1])
 
-        wa_raw = placed([P, PASSES, R], I32, "wa_raw", 6656)
-        nc.sync.dma_start(wa_raw[:], wa_words.rearrange("z p r t -> p z (r t)").bitcast(I32))
-        xw_table = [placed([P, T], U16, "xw_table%d" % z, 10752 + 4096 * z) for z in range(PASSES)]
+        wa_raw = [placed([P, R], I32, "wa_raw%d" % z, (6656, 16896)[z]) for z in range(PASSES)]
+        xw_table = [placed([P, T], U16, "xw_table%d" % z, 8704 + 4096 * z) for z in range(PASSES)]
+        wa_rows = wa_words.rearrange("z p r t -> z p (r t)").bitcast(I32)
+        nc.sync.dma_start(wa_raw[0][:], wa_rows[0])
         for z in range(PASSES):
             nc.sync.dma_start(xw_table[z][:].bitcast(I32), xq_words[z].bitcast(I32))
+        nc.sync.dma_start(wa_raw[1][:], wa_rows[1])
         xs_plane = sb([P, PASSES * J], U8, "xs_plane")
         nc.vector.memset(xs_plane[:].bitcast(I32), 0)
         bias = sb([P, PACK], F32, "bias")
         nc.gpsimd.dma_start(bias[:], b.rearrange("(p t) o -> p (t o)", t=PACK))
-        wb_raw = placed([P, N], U16, "wb_raw", 18944)
-        nc.sync.dma_start(wb_raw[:].bitcast(I32), wb_words[0].bitcast(I32))
 
         xs_picked = sb([P, J], U8, "xs_picked")
         nc.vector.tensor_copy(xs_picked[:], xs_table[:].indirect(list1[:]))
         for q in range(4):
-            nc.scalar.dma_start(
+            (nc.scalar if q % 2 == 0 else nc.sync).dma_start(
                 xs_plane[32 * q : 32 * q + 4, :].rearrange("p (z j) -> p z j", z=PASSES).bitcast(I32),
                 xs_picked[32 * q : 32 * q + 32 : 4, :].bitcast(I32),
             )
@@ -86,35 +86,52 @@ def tile_list_experts_second_opinion_pl_kernel(
             was_raw[:].rearrange("p (z q t) -> p z q t", z=PASSES, t=PACK),
         )
         wa_codes = placed([P, PASSES, PACK, P], I32, "wa_codes", 1536)
-        nc.vector.tensor_copy(
-            wa_codes[:].rearrange("p z t q -> p z q t"), wa_raw[:].rearrange("p z (q t) -> p z q t", t=PACK)
-        )
+
+        def deal_wa(z):
+            nc.vector.tensor_copy(
+                wa_codes[:, z].rearrange("p t q -> p q t"), wa_raw[z][:].rearrange("p (q t) -> p q t", t=PACK)
+            )
+
+        deal_wa(0)
+        wb_raw = placed([P, N], U16, "wb_raw", 7680)
+        nc.sync.dma_start(wb_raw[:].bitcast(I32), wb_words[0].bitcast(I32))
         wbs_raw = placed([P, N], U8, "wbs_raw", 0)
-        nc.vector.memset(wbs_raw[:].bitcast(I32), 0)
+        nc.gpsimd.memset(wbs_raw[:].bitcast(I32), 0)
         for q in range(4):
             nc.sync.dma_start(
                 wbs_raw[32 * q : 32 * q + 4, :].bitcast(I32), wb_scales[0, 4 * q : 4 * q + 4, :].bitcast(I32)
             )
 
+        warm = psum.tile([P, HALF], F32, name="warm", tag="bank7")
+        for u in range(2):
+            nc.tensor.matmul_mx(
+                out=warm[:],
+                lhsT=xw_table[0][:, 0:P].bitcast(FP4X4),
+                lhsT_scale=wa_plane[:, 0, 0, :],
+                rhs=wa_codes[:, 0].rearrange("p t q -> p (t q)").bitcast(FP8X4),
+                rhs_scale=wa_plane[:, 0].rearrange("p t q -> p (t q)"),
+                start=(u == 0),
+                stop=(u == 1),
+            )
+
         hid = [sb([P, J], F32, "hid%d" % t) for t in range(PACK)]
-        xw_picked = [placed([P, PASSES, HALF], U16, "xw_picked%d" % h, (5632, 18944)[h]) for h in range(2)]
+        xw_picked = [placed([P, PASSES, HALF], U16, "xw_picked%d" % h, (5632, 16896)[h]) for h in range(2)]
         for h in range(J // HALF):
             cols = slice(h * HALF, (h + 1) * HALF)
             picked = []
-            if h == 1:
-                wb_codes = sb([P, PACK, P], U16, "wb_codes")
-                nc.vector.tensor_copy(
-                    wb_codes[:].rearrange("p t q -> p q t"), wb_raw[:].rearrange("p (q t) -> p q t", t=PACK)
-                )
             for z in range(PASSES):
                 words = xw_picked[h][:, z, :]
                 nc.vector.tensor_copy(
                     words, xw_table[z][:].indirect(list1[:, h * HALF // 16 : (h + 1) * HALF // 16])
                 )
                 picked.append(words)
-            acc = [psum.tile([P, HALF], F32, name="acc%d%d" % (h, t), tag="bank%d" % (t % 3 if h == 0 else 3 + t)) for t in range(PACK)]
+            if h == 1:
+                nc.vector.tensor_scalar_max(late[0], late[1], 0.0)
             if h == 0:
-                order = [(0, 0), (0, 1), (0, 2), (1, 0), (1, 1), (1, 2), (0, 3), (1, 3)]
+                deal_wa(1)
+            acc = [psum.tile([P, HALF], F32, name="acc%d%d" % (h, t), tag="bank%d" % (4 * h + t)) for t in range(PACK)]
+            if h == 0:
+                order = [(z, t) for z in range(PASSES) for t in range(PACK)]
             else:
                 order = [(z, t) for t in range(PACK) for z in range(PASSES)]
             for z, t in order:
@@ -127,10 +144,16 @@ def tile_list_experts_second_opinion_pl_kernel(
                     start=(z == 0),
                     stop=(z == PASSES - 1),
                 )
-                if z == PASSES - 1:
+                if z == PASSES - 1 and (h, t) == (0, 3):
+                    late = (hid[t][:, cols], acc[t][:])
+                elif z == PASSES - 1:
                     nc.scalar.activation(hid[t][:, cols], acc[t][:], ACT.Relu, bias=zero[:])
 
-        wb_plane = placed([P, PACK, P], U8, "wb_plane", 15872)
+        wb_codes = placed([P, PACK, P], U16, "wb_codes", 12800)
+        nc.vector.tensor_copy(
+            wb_codes[:].rearrange("p t q -> p q t"), wb_raw[:].rearrange("p (q t) -> p q t", t=PACK)
+        )
+        wb_plane = placed([P, PACK, P], U8, "wb_plane", 13824)
         nc.vector.tensor_copy(
             wb_plane[:].rearrange("p t q -> p q t"), wbs_raw[:].rearrange("p (q t) -> p q t", t=PACK)
         )
@@ -145,10 +168,10 @@ def tile_list_experts_second_opinion_pl_kernel(
 
         def gather(c):
             i0, w = CHUNKS[c]
-            if c == 1:
-                hs_rows[c] = placed([P, PACK, w], BF16, "hs_rows1", 20992)
+            if c == 2:
+                hs_rows[c] = placed([P, PACK, w], BF16, "hs_rows2", 20992)
             else:
-                hs_rows[c] = sb([P, PACK, w], BF16, "hs_rows%d" % c, tag="hs_rows0")
+                hs_rows[c] = sb([P, PACK, w], BF16, "hs_rows%d" % c, tag="hs_rows%d" % min(c, 1))
             for t in range(PACK):
                 nc.vector.tensor_copy(hs_rows[c][:, t, :], hid[t][:].indirect(list2[:, i0 // 16 : (i0 + w) // 16]))
 
@@ -169,10 +192,10 @@ def tile_list_experts_second_opinion_pl_kernel(
             nc.vector.quantize_mx(
                 out=hs_codes[c][:].bitcast(FP8X4), scales=hs_plane[c][:], in_=hs_woven[c][:].rearrange("p i t -> p (i t)")
             )
-            per_bank = HALF // w
-            first_bank = (7 + i0 // P) % 8
+            per_bank = 2 if c == last else PACK
+            first_bank = PACK if c == last else c
             banks[c] = [
-                psum.tile([P, per_bank, w], F32, name="res%d%d" % (c, u), tag="bank%d" % ((first_bank + u) % 8))
+                psum.tile([P, per_bank, w], F32, name="res%d%d" % (c, u), tag="bank%d" % (first_bank + u))
                 for u in range(PACK // per_bank)
             ]
             for t in range(PACK):
@@ -190,11 +213,12 @@ def tile_list_experts_second_opinion_pl_kernel(
 
         def drain(c):
             i0, w = CHUNKS[c]
-            per_bank = HALF // w
             y[c] = sb([P, PACK, w], F32, "y%d" % c)
-            for t in range(PACK):
-                nc.scalar.activation(
-                    y[c][:, t, :], banks[c][t // per_bank][:, t % per_bank, :], ACT.Identity, bias=bias[:, t : t + 1]
+            for t in range(2 if c == last else PACK):
+                nc.scalar.activation(y[c][:, t, :], banks[c][0][:, t, :], ACT.Identity, bias=bias[:, t : t + 1])
+            if c == last:
+                nc.vector.tensor_tensor(
+                    y[c][:, 2:4, :], banks[c][1][:], bias[:, 2:4].unsqueeze(2).to_broadcast([P, 2, w]), ALU.add
                 )
             nc.sync.dma_start(out_rows[:, :, i0 : i0 + w], y[c][:])
 
@@ -209,27 +233,37 @@ def tile_list_experts_second_opinion_pl_kernel(
                 scales=y_plane[:, i0 : i0 + w],
                 in_=woven.rearrange("p i t -> p (i t)"),
             )
+
+        def store_words(i0, w):
             nc.sync.dma_start(out_words[:, i0 : i0 + w], y_codes[:, i0 : i0 + w].bitcast(I32))
 
+        first = sb([P, 256, PACK], BF16, "y_woven0")
+        rest = sb([P, 256, PACK], BF16, "y_woven1")
         gather(0)
         weave(0)
         gather(1)
         weave(1)
-        multiply(0)
         gather(2)
-        multiply(1)
         weave(2)
-        multiply(2)
+        multiply(0)
+        multiply(1)
         drain(0)
+        gather(3)
+        multiply(2)
+        weave(3)
+        weave_y(0, first[:, 0:128, :])
+        multiply(3)
         drain(1)
         drain(2)
-        first = sb([P, 256, PACK], BF16, "y_woven0")
-        rest = sb([P, 256, PACK], BF16, "y_woven1")
-        weave_y(0, first[:])
-        weave_y(1, rest[:, 0:128, :])
+        weave_y(1, first[:, 128:256, :])
         hand_on(0, 256, first[:])
-        weave_y(2, rest[:, 128:256, :])
-        hand_on(256, 256, rest[:])
+        store_words(0, 256)
+        drain(3)
+        weave_y(2, rest[:, 0:128, :])
+        weave_y(3, rest[:, 128:256, :])
+        hand_on(256, 128, rest[:, 0:128, :])
+        hand_on(384, 128, rest[:, 128:256, :])
+        store_words(256, 256)
         for q in range(4):
             eng = nc.sync if q < 2 else nc.scalar
             eng.dma_start(out_2[0, 4 * q : 4 * q + 4, :].bitcast(I32), y_plane[32 * q : 32 * q + 4, :].bitcast(I32))

from contextlib import ExitStack

import concourse.mybir as mybir

K, T, J, I, R, N = 1024, 2048, 1024, 512, 512, 512
FLOPS = 2 * K * R * J + 2 * R * N * I

F32 = mybir.dt.float32
BF16 = mybir.dt.bfloat16
I32 = mybir.dt.int32
U32 = mybir.dt.uint32
U16 = mybir.dt.uint16
U8 = mybir.dt.uint8
FP8X4 = mybir.dt.float8_e4m3fn_x4
FP4X4 = mybir.dt.float4_e2m1fn_x4
ACT = mybir.ActivationFunctionType
ALU = mybir.AluOpType

P = 128
PACK = 4
PASSES = K // (P * PACK)
HALF = 512
CHUNKS = [(0, 128), (128, 128), (256, 128), (384, 128)]


def tile_list_experts_second_opinion_pl_kernel(
    tc, xq_words, xq_scales, wa_words, wa_scales, wb_words, wb_scales, b, offs, offs2, out_0, out_1, out_2
):
    nc = tc.nc
    with ExitStack() as ctx:
        keep = ctx.enter_context(tc.tile_pool(name="keep", bufs=1))
        reuse = ctx.enter_context(tc.tile_pool(name="reuse", bufs=1))
        psum = ctx.enter_context(tc.psum_pool(name="psum", bufs=1))

        def sb(shape, dtype, name, tag=None):
            return keep.tile(shape, dtype, name=name, tag=tag or name, align_bytes=64)

        def placed(shape, dtype, name, offset):
            return reuse.tile(shape, dtype, name=name, offset=offset, align_bytes=64)

        list1 = keep.tile([P, J // 16], U16, name="list1")
        list2 = keep.tile([P, I // 16], U16, name="list2")

        xs_table = placed([P, T], U8, "xs_table", 0)
        nc.vector.memset(xs_table[:].bitcast(I32), 0)
        nc.sync.dma_start(list1[:], offs)
        nc.sync.dma_start(list2[:], offs2)
        nc.sync.dma_start(xs_table[0:P:4, :].bitcast(I32), xq_scales.rearrange("z v t -> v z t").bitcast(I32))
        was_raw = placed([P, PASSES * R], U8, "was_raw", 5632)
        nc.vector.memset(was_raw[:].bitcast(I32), 0)
        for q in range(4):
            nc.sync.dma_start(
                was_raw[32 * q : 32 * q + 4, :].rearrange("p (z r) -> p z r", z=PASSES).bitcast(I32),
                wa_scales[:, 4 * q : 4 * q + 4, :].rearrange("z s r -> s z r").bitcast(I32),
            )
        zero = placed([P, 1], F32, "zero", 20992)
        zero_a = reuse.tile([P, 16], F32, name="zero_a", offset=8704 - 32, align_bytes=32)
        zero_b = reuse.tile([P, 16], F32, name="zero_b", offset=16896 - 32, align_bytes=32)
        nc.gpsimd.memset(zero_a[:], 0.0)
        nc.gpsimd.memset(zero_b[:], 0.0)
        nc.scalar.activation(zero[:], zero_a[:, 0:1], ACT.Relu, bias=zero_b[:, 0:1])

        wa_raw = [placed([P, R], I32, "wa_raw%d" % z, (6656, 16896)[z]) for z in range(PASSES)]
        xw_table = [placed([P, T], U16, "xw_table%d" % z, 8704 + 4096 * z) for z in range(PASSES)]
        wa_rows = wa_words.rearrange("z p r t -> z p (r t)").bitcast(I32)
        nc.sync.dma_start(wa_raw[0][:], wa_rows[0])
        for z in range(PASSES):
            nc.sync.dma_start(xw_table[z][:].bitcast(I32), xq_words[z].bitcast(I32))
        nc.sync.dma_start(wa_raw[1][:], wa_rows[1])
        xs_plane = sb([P, PASSES * J], U8, "xs_plane")
        nc.vector.memset(xs_plane[:].bitcast(I32), 0)
        bias = sb([P, PACK], F32, "bias")
        nc.gpsimd.dma_start(bias[:], b.rearrange("(p t) o -> p (t o)", t=PACK))

        xs_picked = sb([P, J], U8, "xs_picked")
        nc.vector.tensor_copy(xs_picked[:], xs_table[:].indirect(list1[:]))
        for q in range(4):
            (nc.scalar if q % 2 == 0 else nc.sync).dma_start(
                xs_plane[32 * q : 32 * q + 4, :].rearrange("p (z j) -> p z j", z=PASSES).bitcast(I32),
                xs_picked[32 * q : 32 * q + 32 : 4, :].bitcast(I32),
            )

        wa_plane = placed([P, PASSES, PACK, P], U8, "wa_plane", 512)
        nc.vector.tensor_copy(
            wa_plane[:].rearrange("p z t q -> p z q t"),
            was_raw[:].rearrange("p (z q t) -> p z q t", z=PASSES, t=PACK),
        )
        wa_codes = placed([P, PASSES, PACK, P], I32, "wa_codes", 1536)

        def deal_wa(z):
            nc.vector.tensor_copy(
                wa_codes[:, z].rearrange("p t q -> p q t"), wa_raw[z][:].rearrange("p (q t) -> p q t", t=PACK)
            )

        deal_wa(0)
        wb_raw = placed([P, N], U16, "wb_raw", 7680)
        nc.sync.dma_start(wb_raw[:].bitcast(I32), wb_words[0].bitcast(I32))
        wbs_raw = placed([P, N], U8, "wbs_raw", 0)
        nc.gpsimd.memset(wbs_raw[:].bitcast(I32), 0)
        for q in range(4):
            nc.sync.dma_start(
                wbs_raw[32 * q : 32 * q + 4, :].bitcast(I32), wb_scales[0, 4 * q : 4 * q + 4, :].bitcast(I32)
            )

        warm = psum.tile([P, HALF], F32, name="warm", tag="bank7")
        for u in range(2):
            nc.tensor.matmul_mx(
                out=warm[:],
                lhsT=xw_table[0][:, 0:P].bitcast(FP4X4),
                lhsT_scale=wa_plane[:, 0, 0, :],
                rhs=wa_codes[:, 0].rearrange("p t q -> p (t q)").bitcast(FP8X4),
                rhs_scale=wa_plane[:, 0].rearrange("p t q -> p (t q)"),
                start=(u == 0),
                stop=(u == 1),
            )

        hid = [sb([P, J], F32, "hid%d" % t) for t in range(PACK)]
        xw_picked = [placed([P, PASSES, HALF], U16, "xw_picked%d" % h, (5632, 16896)[h]) for h in range(2)]
        for h in range(J // HALF):
            cols = slice(h * HALF, (h + 1) * HALF)
            picked = []
            for z in range(PASSES):
                words = xw_picked[h][:, z, :]
                nc.vector.tensor_copy(
                    words, xw_table[z][:].indirect(list1[:, h * HALF // 16 : (h + 1) * HALF // 16])
                )
                picked.append(words)
            if h == 1:
                nc.vector.tensor_scalar_max(late[0], late[1], 0.0)
            if h == 0:
                deal_wa(1)
            acc = [psum.tile([P, HALF], F32, name="acc%d%d" % (h, t), tag="bank%d" % (4 * h + t)) for t in range(PACK)]
            if h == 0:
                order = [(z, t) for z in range(PASSES) for t in range(PACK)]
            else:
                order = [(z, t) for t in range(PACK) for z in range(PASSES)]
            for z, t in order:
                nc.tensor.matmul_mx(
                    out=acc[t][:],
                    lhsT=wa_codes[:, z, t, :].bitcast(FP8X4),
                    lhsT_scale=wa_plane[:, z, t, :],
                    rhs=picked[z].bitcast(FP4X4),
                    rhs_scale=xs_plane[:, z * J + h * HALF : z * J + (h + 1) * HALF],
                    start=(z == 0),
                    stop=(z == PASSES - 1),
                )
                if z == PASSES - 1 and (h, t) == (0, 3):
                    late = (hid[t][:, cols], acc[t][:])
                elif z == PASSES - 1:
                    nc.scalar.activation(hid[t][:, cols], acc[t][:], ACT.Relu, bias=zero[:])

        wb_codes = placed([P, PACK, P], U16, "wb_codes", 12800)
        nc.vector.tensor_copy(
            wb_codes[:].rearrange("p t q -> p q t"), wb_raw[:].rearrange("p (q t) -> p q t", t=PACK)
        )
        wb_plane = placed([P, PACK, P], U8, "wb_plane", 13824)
        nc.vector.tensor_copy(
            wb_plane[:].rearrange("p t q -> p q t"), wbs_raw[:].rearrange("p (q t) -> p q t", t=PACK)
        )

        y_codes = sb([P, I], U32, "y_codes")
        y_plane = sb([P, I], U8, "y_plane")
        out_rows = out_0.rearrange("(p t) i -> p t i", t=PACK)
        out_words = out_1[0].rearrange("p i t -> p (i t)").bitcast(I32)
        last = len(CHUNKS) - 1

        hs_rows, hs_woven, hs_codes, hs_plane, banks, y = {}, {}, {}, {}, {}, {}

        def gather(c):
            i0, w = CHUNKS[c]
            if c == 2:
                hs_rows[c] = placed([P, PACK, w], BF16, "hs_rows2", 20992)
            else:
                hs_rows[c] = sb([P, PACK, w], BF16, "hs_rows%d" % c, tag="hs_rows%d" % min(c, 1))
            for t in range(PACK):
                nc.vector.tensor_copy(hs_rows[c][:, t, :], hid[t][:].indirect(list2[:, i0 // 16 : (i0 + w) // 16]))

        def weave(c):
            i0, w = CHUNKS[c]
            hs_woven[c] = sb([P, w, PACK], BF16, "hs_woven%d" % c)
            dst = hs_woven[c][:].rearrange("p (g i) t -> p g t i", i=4)
            src = hs_rows[c][:].rearrange("p t (g i) -> p g t i", i=4)
            if c == last:
                nc.vector.tensor_copy(dst, src)
            else:
                nc.scalar.copy(dst, src)

        def multiply(c):
            i0, w = CHUNKS[c]
            hs_codes[c] = sb([P, w], U32, "hs_codes%d" % c)
            hs_plane[c] = sb([P, w], U8, "hs_plane%d" % c)
            nc.vector.quantize_mx(
                out=hs_codes[c][:].bitcast(FP8X4), scales=hs_plane[c][:], in_=hs_woven[c][:].rearrange("p i t -> p (i t)")
            )
            per_bank = 2 if c == last else PACK
            first_bank = PACK if c == last else c
            banks[c] = [
                psum.tile([P, per_bank, w], F32, name="res%d%d" % (c, u), tag="bank%d" % (first_bank + u))
                for u in range(PACK // per_bank)
            ]
            for t in range(PACK):
                nc.tensor.matmul_mx(
                    out=banks[c][t // per_bank][:, t % per_bank, :],
                    lhsT=wb_codes[:, t, :].bitcast(FP4X4),
                    lhsT_scale=wb_plane[:, t, :],
                    rhs=hs_codes[c][:].bitcast(FP8X4),
                    rhs_scale=hs_plane[c][:],
                    start=True,
                    stop=True,
                )

        y_woven = {}

        def drain(c):
            i0, w = CHUNKS[c]
            y[c] = sb([P, PACK, w], F32, "y%d" % c)
            for t in range(2 if c == last else PACK):
                nc.scalar.activation(y[c][:, t, :], banks[c][0][:, t, :], ACT.Identity, bias=bias[:, t : t + 1])
            if c == last:
                nc.vector.tensor_tensor(
                    y[c][:, 2:4, :], banks[c][1][:], bias[:, 2:4].unsqueeze(2).to_broadcast([P, 2, w]), ALU.add
                )
            nc.sync.dma_start(out_rows[:, :, i0 : i0 + w], y[c][:])

        def weave_y(c, dst):
            nc.vector.tensor_copy(
                dst.rearrange("p (g i) t -> p g t i", i=4), y[c][:].rearrange("p t (g i) -> p g t i", i=4)
            )

        def hand_on(i0, w, woven):
            nc.vector.quantize_mx(
                out=y_codes[:, i0 : i0 + w].bitcast(FP8X4),
                scales=y_plane[:, i0 : i0 + w],
                in_=woven.rearrange("p i t -> p (i t)"),
            )

        def store_words(i0, w):
            nc.sync.dma_start(out_words[:, i0 : i0 + w], y_codes[:, i0 : i0 + w].bitcast(I32))

        first = sb([P, 256, PACK], BF16, "y_woven0")
        rest = sb([P, 256, PACK], BF16, "y_woven1")
        gather(0)
        weave(0)
        gather(1)
        weave(1)
        gather(2)
        weave(2)
        multiply(0)
        multiply(1)
        drain(0)
        gather(3)
        multiply(2)
        weave(3)
        weave_y(0, first[:, 0:128, :])
        multiply(3)
        drain(1)
        drain(2)
        weave_y(1, first[:, 128:256, :])
        hand_on(0, 256, first[:])
        store_words(0, 256)
        drain(3)
        weave_y(2, rest[:, 0:128, :])
        weave_y(3, rest[:, 128:256, :])
        hand_on(256, 128, rest[:, 0:128, :])
        hand_on(384, 128, rest[:, 128:256, :])
        store_words(256, 256)
        for q in range(4):
            eng = nc.sync if q < 2 else nc.scalar
            eng.dma_start(out_2[0, 4 * q : 4 * q + 4, :].bitcast(I32), y_plane[32 * q : 32 * q + 4, :].bitcast(I32))
